import numpy as np
import ml_dtypes


def mxq(x, axis, fmt="e4m3"):
    dtype, down = {"e4m3": (ml_dtypes.float8_e4m3fn, 7), "e5m2": (ml_dtypes.float8_e5m2, 14)}[fmt]
    v = np.moveaxis(np.asarray(x, np.float32).astype(ml_dtypes.bfloat16).astype(np.float64), axis, -1)
    blocks = v.reshape(v.shape[:-1] + (-1, 32))
    amax = np.abs(blocks).max(-1, keepdims=True)
    byte = np.maximum(np.where(amax > 0, np.frexp(amax)[1] - 1 + 127, 0) - down, 1)
    scale = np.exp2(byte - 127.0)
    codes = (blocks / scale).astype(np.float32).astype(dtype).astype(np.float64)
    return np.moveaxis((codes * scale).reshape(v.shape), -1, axis)


WIDE = False


def mx_kscale(k):
    if not WIDE:
        return np.ones(k)
    levels = np.array([10, -10, 5, -5, 0])
    if k % 512:
        return np.exp2(np.random.permutation(np.resize(levels, k // 32))).repeat(32)
    a = np.empty((k // 512, 16))
    for p in range(k // 512):
        a[p, :8] = np.random.permutation(np.resize(levels, 8))
        for g in range(8):
            far = levels[np.abs(levels - a[p, g]) >= 10]
            a[p, g + 8] = far[np.random.randint(len(far))]
    return np.exp2(a.ravel()).repeat(32)


def f64(x):
    return np.asarray(x).astype(np.float64)


def striped(idx):
    return np.tile(idx.reshape(-1, 16).T, (8, 1)).astype(np.uint16)


def unstriped(offs):
    return offs[:16].T.reshape(-1).astype(np.int64)


def striped8(idx):
    return np.concatenate([x.reshape(-1, 16).T for x in idx]).astype(np.uint16)


def runs(offs, k):
    lists = np.stack([offs[16 * r : 16 * r + 16].T.reshape(-1) for r in range(8)]).astype(np.int64)
    return lists[np.arange(k) % 512 // 64]


def pack_weight(w):
    k, n = w.shape
    w = f64(np.asarray(w, np.float32).astype(ml_dtypes.bfloat16)).reshape(k // 32, 32, n)
    amax = np.abs(w).max(1)
    byte = np.clip(np.where(amax > 0, np.frexp(amax)[1] - 1 + 127 - 7, 1), 1, 254)
    scaled = (w * np.exp2(127.0 - byte)[:, None, :]).reshape(k, n).astype(np.float32)
    words = np.ascontiguousarray(scaled.reshape(k // 512, 128, 4, n).transpose(0, 1, 3, 2)).astype(ml_dtypes.float8_e4m3fn).view(np.uint8)
    return words, np.ascontiguousarray(byte.astype(np.uint8).reshape(k // 512, 16, n))


def unpack_weight(words, scales):
    g, p, n, _ = words.shape
    vals = np.ascontiguousarray(words).view(ml_dtypes.float8_e4m3fn).astype(np.float64) * np.repeat(np.exp2(scales.astype(np.float64) - 127.0), 8, axis=1)[..., None]
    return vals.transpose(0, 1, 3, 2).reshape(g * 512, n)


E2M1 = np.array([0.0, 0.5, 1.0, 1.5, 2.0, 3.0, 4.0, 6.0, -0.0, -0.5, -1.0, -1.5, -2.0, -3.0, -4.0, -6.0])


def pack_fp4(w):
    k, n = w.shape
    w = f64(np.asarray(w, np.float32).astype(ml_dtypes.bfloat16)).reshape(k // 32, 32, n)
    amax = np.abs(w).max(1)
    mant, ex = np.frexp(amax / 6.0)
    byte = np.clip(np.where(amax > 0, np.where(mant > 0.5, ex, ex - 1) + 127, 1), 1, 254)
    scaled = (w * np.exp2(127.0 - byte)[:, None, :]).reshape(k, n).astype(np.float32)
    c = np.ascontiguousarray(scaled.reshape(k // 512, 128, 4, n).transpose(0, 1, 3, 2)).astype(ml_dtypes.float4_e2m1fn).view(np.uint8) & 0xF
    words = (c[..., 0::2] | (c[..., 1::2] << 4)).reshape(k // 512, 128, 2 * n)
    return np.ascontiguousarray(words), np.ascontiguousarray(byte.astype(np.uint8).reshape(k // 512, 16, n))


def unpack_fp4(words, scales):
    g, _, n = scales.shape
    words = np.ascontiguousarray(words).reshape(g, 128, n, 2)
    nib = np.empty((g, 128, n, 4), np.uint8)
    nib[..., 0::2] = words & 0xF
    nib[..., 1::2] = words >> 4
    vals = E2M1[nib] * np.repeat(np.exp2(scales.astype(np.float64) - 127.0), 8, axis=1)[..., None]
    return vals.transpose(0, 1, 3, 2).reshape(g * 512, n)


def planes(y):
    n, m = y.shape
    v = y.astype(np.float32).astype(ml_dtypes.bfloat16).astype(np.float64).reshape(n // 32, 32, m)
    top = np.abs(v).max(1)
    byte = np.clip(np.where(top > 0, np.frexp(top)[1] - 1 + 127 - 7, 1), 1, 254)
    codes = (v * np.exp2(127.0 - byte)[:, None, :]).reshape(n, m).astype(np.float32).astype(ml_dtypes.float8_e4m3fn).view(np.uint8)
    words = codes.reshape(n // 512, 128, 4, m).transpose(0, 1, 3, 2)
    return np.ascontiguousarray(words), np.ascontiguousarray(byte.astype(np.uint8).reshape(n // 512, 16, m))


K, T, S, V, N, H = 512, 2048, 512, 256, 512, 512
P = 2 ** 7


def setup_inputs():
    n = np.random.standard_normal
    s = mx_kscale(K)[:, None]
    u = mx_kscale(S)
    packed_xT = pack_weight(n((K, T)) * s)
    packed_w1 = pack_fp4(n((S, N)) / np.sqrt(S) / u[:, None])
    perm = np.stack([np.random.permutation(H) for _ in range(8)])
    return {
        "x_words": packed_xT[0],
        "x_scales": packed_xT[1],
        "wa": (n((K, H)) / np.sqrt(K) / s).astype(np.float32),
        "cs": np.tile(np.random.uniform(0.3, 0.9, V), (P, 1)).astype(np.float32),
        "sn": np.tile(np.random.uniform(-0.9, -0.3, V), (P, 1)).astype(np.float32),
        "gt": (np.random.uniform(0.5, 1.5, (S, 1)) * u[:, None]).astype(np.float32),
        "w1_words": packed_w1[0],
        "w1_scales": packed_w1[1],
        "offs": striped(np.random.permutation(T)[:S]),
        "la": striped8(perm[:, :V]),
        "lb": striped8(perm[:, V:]),
    }


def reference(x_words, x_scales, wa, cs, sn, gt, w1_words, w1_scales, offs, la, lb):
    xq = unpack_weight(x_words, x_scales)[:, unstriped(offs)]
    y = xq.T @ mxq(f64(wa), 0, "e4m3")
    a = y[np.arange(S)[:, None], runs(la, S)]
    b = y[np.arange(S)[:, None], runs(lb, S)]
    r2 = f64(sn)[:1] * a + f64(cs)[:1] * b
    r1 = f64(cs)[:1] * a - (f64(sn)[:1] * b)
    p = np.zeros((S, H))
    p[np.arange(S)[:, None], runs(la, S)] = r1
    d = p.copy()
    d[np.arange(S)[:, None], runs(lb, S)] = r2
    z = f64(gt) * d
    out_0 = unpack_fp4(w1_words, w1_scales).T @ mxq(z, 0, "e4m3")
    return (out_0,) + planes(out_0)

from contextlib import ExitStack

import concourse.mybir as mybir
from concourse.masks import make_identity

FLOPS = 2 * 2 * 512 * 512 * 512

F32 = mybir.dt.float32
BF16 = mybir.dt.bfloat16
I32 = mybir.dt.int32
U32 = mybir.dt.uint32
U16 = mybir.dt.uint16
U8 = mybir.dt.uint8
FP8X4 = mybir.dt.float8_e4m3fn_x4
FP4X4 = mybir.dt.float4_e2m1fn_x4
COPY = mybir.ActivationFunctionType.Copy

P = 128
PACK = 4
T = 2048
S = 512
H = 512
V = 256
M = 512
WA_CHUNK = 128
HALF = 256
ORDER = (2, 0, 1, 3)
OUT_CHUNK = 128


def interleave(copy, dst, src):
    copy(dst.rearrange("p (c i) t -> p c t i", i=4), src.rearrange("p t (c i) -> p c t i", i=4))


def tile_picked_featrot_none_po_kernel(
    tc, x_words, x_scales, wa, cs, sn, gt, w1_words, w1_scales, offs, la, lb, out_0, out_1, out_2
):
    nc = tc.nc

    def vector_copy(dst, src):
        nc.vector.tensor_copy(out=dst, in_=src)

    def scalar_copy(dst, src):
        nc.scalar.activation(out=dst, in_=src, func=COPY)

    with ExitStack() as ctx:
        keep = ctx.enter_context(tc.tile_pool(name="keep", bufs=1))
        psum = ctx.enter_context(tc.psum_pool(name="psum", bufs=1))
        reuse = ctx.enter_context(tc.tile_pool(name="reuse", bufs=1))

        offs_sb = keep.tile([P, S // 16], U16, name="offs_sb")
        la_sb = keep.tile([P, V // 16], U16, name="la_sb")
        lb_sb = keep.tile([P, V // 16], U16, name="lb_sb")
        xw = keep.tile([P, T], U32, name="xw", align_bytes=64)
        xs = keep.tile([P, T], U8, name="xs", align_bytes=64)
        w1w = keep.tile([P, 2 * M], U8, name="w1w", align_bytes=64)
        w1s = keep.tile([P, M], U8, name="w1s", align_bytes=64)
        gt_sb = keep.tile([P, PACK], F32, name="gt_sb")
        cs_sb = keep.tile([P, 2], F32, name="cs_sb")
        sn_sb = keep.tile([P, 2], F32, name="sn_sb")
        nsn_sb = keep.tile([P, 2], F32, name="nsn_sb")
        ident = keep.tile([P, P], F32, name="ident")

        nc.vector.memset(xs[:].bitcast(I32), 0)
        nc.vector.memset(w1s[:].bitcast(I32), 0)
        make_identity(nc, ident[:])

        nc.sync.dma_start(offs_sb[:], offs)
        nc.sync.dma_start(xw[:].bitcast(I32), x_words[0].rearrange("p n r -> p (n r)").bitcast(I32))
        for q in range(4):
            nc.sync.dma_start(xs[32 * q : 32 * q + 4, :].bitcast(I32), x_scales[0, 4 * q : 4 * q + 4, :].bitcast(I32))
        wa_rows = wa.rearrange("(p j) n -> p j n", j=PACK)
        wa_raw = []
        for c0 in range(0, H, WA_CHUNK):
            raw = keep.tile([P, PACK, WA_CHUNK], F32, name=f"wa_raw{c0}")
            nc.sync.dma_start(raw[:], wa_rows[:, :, c0 : c0 + WA_CHUNK])
            wa_raw.append(raw)
        nc.sync.dma_start(gt_sb[:], gt.rearrange("(p t) o -> p (t o)", t=PACK))
        nc.sync.dma_start(la_sb[:], la)
        nc.sync.dma_start(lb_sb[:], lb)
        nc.sync.dma_start(w1w[:].bitcast(I32), w1_words[0].bitcast(I32))
        for q in range(4):
            nc.sync.dma_start(w1s[32 * q : 32 * q + 4, :].bitcast(I32), w1_scales[0, 4 * q : 4 * q + 4, :].bitcast(I32))
        with nc.allow_non_contiguous_dma(reason="one factor to a partition"):
            nc.sync.dma_start(cs_sb[:], cs[0:1, :].rearrange("o (b p) -> p (o b)", p=P))
            nc.sync.dma_start(sn_sb[:], sn[0:1, :].rearrange("o (b p) -> p (o b)", p=P))

        xg = keep.tile([P, PACK, P], U32, name="xg", align_bytes=64)
        nc.vector.tensor_copy(out=xg[:].rearrange("p t m -> p m t"), in_=xw[:].indirect(offs_sb[:]))
        xsg = keep.tile([P, S], U8, name="xsg", align_bytes=64)
        nc.vector.tensor_copy(out=xsg[:], in_=xs[:].indirect(offs_sb[:]))
        xsd = keep.tile([P, PACK, P], U8, name="xsd", align_bytes=64)
        nc.vector.tensor_copy(out=xsd[:], in_=xsg[:].rearrange("p (m t) -> p t m", t=PACK))

        banks = {t: psum.tile([P, H], F32, name=f"y{t}", tag="big", bufs=4) for t in ORDER}
        wa_codes = keep.tile([P, H], U32, name="wa_codes", align_bytes=64)
        wa_scales = keep.tile([P, H], U8, name="wa_scales", align_bytes=64)
        for h in range(2):
            grouped = reuse.tile([P, HALF, PACK], BF16, name=f"wa_bf{h}", align_bytes=64, offset=2048 * h)
            for i in range(2):
                interleave(scalar_copy, grouped[:, i * WA_CHUNK : (i + 1) * WA_CHUNK, :], wa_raw[2 * h + i][:])
            cols = slice(h * HALF, (h + 1) * HALF)
            nc.vector.quantize_mx(out=wa_codes[:, cols].bitcast(FP8X4), scales=wa_scales[:, cols], in_=grouped[:].rearrange("p n t -> p (n t)"))
        for t in ORDER:
            width = HALF if t == ORDER[0] else H
            for c0 in range(0, H, width):
                cols = slice(c0, c0 + width)
                nc.tensor.matmul_mx(
                    out=banks[t][:, cols], lhsT=xg[:, t, :].bitcast(FP8X4), lhsT_scale=xsd[:, t, :],
                    rhs=wa_codes[:, cols].bitcast(FP8X4), rhs_scale=wa_scales[:, cols], start=True, stop=True,
                )

        w1wd = reuse.tile([P, PACK, 2 * P], U8, name="w1wd", align_bytes=64, offset=2048)
        nc.vector.tensor_copy(
            out=w1wd[:].rearrange("p t (m e) -> p t m e", e=2),
            in_=w1w[:].rearrange("p (m t e) -> p t m e", t=PACK, e=2),
        )
        w1sd = reuse.tile([P, PACK, P], U8, name="w1sd", align_bytes=64, offset=3072)
        nc.vector.tensor_copy(out=w1sd[:], in_=w1s[:].rearrange("p (m t) -> p t m", t=PACK))

        y = {}
        for t in ORDER:
            y[t] = keep.tile([P, H], F32, name=f"y_sb{t}")
            nc.scalar.activation(out=y[t][:], in_=banks[t][:], func=COPY, scale=gt_sb[:, t : t + 1])
        nc.scalar.activation(out=nsn_sb[:], in_=sn_sb[:], func=COPY, scale=-1.0)

        ab = {}
        for t in ORDER:
            ab[t] = keep.tile([P, 2, V], F32, name=f"ab{t}")
            nc.vector.tensor_copy(out=ab[t][:, 0, :], in_=y[t][:].indirect(la_sb[:]))
            nc.vector.tensor_copy(out=ab[t][:, 1, :], in_=y[t][:].indirect(lb_sb[:]))

        r = {}
        d = {}

        def rotate(t):
            turned = psum.tile([P, 2, 2, P], F32, name=f"turned{t}", tag="turned", bufs=2)
            for b in range(2):
                for side in range(2):
                    nc.tensor.transpose(turned[:, b, side, :], ab[t][:, side, b * P : (b + 1) * P], ident[:])
            by_cs = keep.tile([P, 2, 2, P], F32, name=f"by_cs{t}", tag="by_cs", bufs=1)
            by_sn = keep.tile([P, 2, 2, P], F32, name=f"by_sn{t}", tag="by_sn", bufs=1, align_bytes=64)
            for b in range(2):
                nc.scalar.activation(out=by_cs[:, b, :, :], in_=turned[:, b, :, :], func=COPY, scale=cs_sb[:, b : b + 1])
                nc.scalar.activation(out=by_sn[:, b, 1, :], in_=turned[:, b, 1, :], func=COPY, scale=nsn_sb[:, b : b + 1])
            for b in range(2):
                nc.scalar.activation(out=by_sn[:, b, 0, :], in_=turned[:, b, 0, :], func=COPY, scale=sn_sb[:, b : b + 1])
            for side in range(2):
                summed = psum.tile([P, 2, P], F32, name=f"summed{t}{side}", tag="summed", bufs=2)
                for b in range(2):
                    nc.tensor.matmul(summed[:, b, :], by_cs[:, b, side, :], ident[:], start=True, stop=False, is_transpose=True)
                    nc.tensor.matmul(summed[:, b, :], by_sn[:, b, 1 - side, :], ident[:], start=False, stop=True, is_transpose=True)
                r[t, side] = keep.tile([P, V], F32, name=f"r{t}{side}")
                nc.scalar.copy(out=r[t, side][:], in_=summed[:].rearrange("p b m -> p (b m)"))

        def scatter(t):
            d[t] = keep.tile([P, H], F32, name=f"d{t}", tag="d", bufs=3)
            nc.vector.tensor_copy(out=d[t][:].indirect(la_sb[:]), in_=r[t, 0][:])
            nc.vector.tensor_copy(out=d[t][:].indirect(lb_sb[:]), in_=r[t, 1][:])

        def regroup(copy, t, c0, c1):
            copy(z[:, c0:c1, t], d[t][:, c0:c1])

        t0, t1, t2, t3 = ORDER
        for t in ORDER:
            rotate(t)
        z = keep.tile([P, H, PACK], BF16, name="z", tag="by_sn", bufs=1, align_bytes=64)
        chunks = [(c, c + OUT_CHUNK) for c in range(0, H, OUT_CHUNK)]
        for t in (t0, t1, t2):
            scatter(t)
            regroup(scalar_copy, t, 0, H)
        scatter(t3)

        z_codes = keep.tile([P, H], U32, name="z_codes", align_bytes=64)
        z_scales = keep.tile([P, H], U8, name="z_scales", align_bytes=64)
        o_codes = keep.tile([P, H], U32, name="o_codes", align_bytes=64)
        o_scales = keep.tile([P, H], U8, name="o_scales", align_bytes=64)
        out_rows = out_0.rearrange("(p t) n -> p t n", t=PACK)
        words_out = out_1[0].rearrange("p n r -> p (n r)").bitcast(I32)
        o_sb = {}
        o_bf = {}

        def second_product(c0, c1):
            nc.vector.quantize_mx(
                out=z_codes[:, c0:c1].bitcast(FP8X4), scales=z_scales[:, c0:c1],
                in_=z[:, c0:c1, :].rearrange("p n t -> p (n t)"),
            )
            acc = psum.tile([P, PACK, c1 - c0], F32, name=f"acc{c0}", tag="big", bufs=4)
            for t in range(PACK):
                nc.tensor.matmul_mx(
                    out=acc[:, t, :], lhsT=w1wd[:, t, :].bitcast(FP4X4), lhsT_scale=w1sd[:, t, :],
                    rhs=z_codes[:, c0:c1].bitcast(FP8X4), rhs_scale=z_scales[:, c0:c1], start=True, stop=True,
                )
            o_sb[c0] = keep.tile([P, PACK, c1 - c0], F32, name=f"o_sb{c0}")
            nc.scalar.copy(out=o_sb[c0][:], in_=acc[:])
            nc.sync.dma_start(out_rows[:, :, c0:c1], o_sb[c0][:])

        def round_out(c0, c1):
            o_bf[c0] = keep.tile([P, c1 - c0, PACK], BF16, name=f"o_bf{c0}", align_bytes=64)
            interleave(vector_copy, o_bf[c0][:], o_sb[c0][:])

        def planes(c0, c1):
            nc.vector.quantize_mx(
                out=o_codes[:, c0:c1].bitcast(FP8X4), scales=o_scales[:, c0:c1],
                in_=o_bf[c0][:].rearrange("p n t -> p (n t)"),
            )

        regroup(vector_copy, t3, *chunks[0])
        regroup(vector_copy, t3, *chunks[1])
        regroup(scalar_copy, t3, *chunks[2])
        regroup(scalar_copy, t3, *chunks[3])
        for chunk in chunks:
            second_product(*chunk)
        round_out(*chunks[0])
        for i, chunk in enumerate(chunks):
            if i + 1 < len(chunks):
                round_out(*chunks[i + 1])
            planes(*chunk)
            if i % 2 == 1:
                c0, c1 = chunks[i - 1][0], chunk[1]
                nc.sync.dma_start(words_out[:, c0:c1], o_codes[:, c0:c1].bitcast(I32))
        for q in range(4):
            queue = nc.scalar if q % 2 else nc.sync
            queue.dma_start(out_2[0, 4 * q : 4 * q + 4, :].bitcast(I32), o_scales[32 * q : 32 * q + 4, :].bitcast(I32))
